import numpy as np
import ml_dtypes

BF16 = ml_dtypes.bfloat16


def bf(x):
    return np.asarray(x, np.float32).astype(BF16)


def f32(x):
    return np.asarray(x, np.float32)


def f64(x):
    return np.asarray(x).astype(np.float64)


def striped(idx):
    return np.tile(idx.reshape(-1, 16).T, (8, 1))


S, K, M, N = 256, 512, 256, 192


def setup_inputs():
    return {"base": bf(np.random.standard_normal((M, S))), "x": bf(np.random.standard_normal((K, N))), "w": bf(np.random.standard_normal((K, M)) / np.sqrt(K)), "offs": striped(np.random.permutation(S)[:N])}


def reference(base, x, w, offs):
    idx = offs[:16].T.reshape(-1)
    z = f64(base).copy()
    z[:, idx] += f64(w).T @ f64(x)
    return z

@@ -1,0 +1,56 @@
+import concourse.mybir as mybir
+from concourse.masks import make_identity
+
+P = 128
+S = 256
+N = 192
+K = 512
+M = 256
+KB = K // P
+MB = M // P
+
+FLOPS = 2 * K * M * N
+
+BF16 = mybir.dt.bfloat16
+F32 = mybir.dt.float32
+U16 = mybir.dt.uint16
+
+
+def tile_scatter_matmul_kernel(tc, base, x, w, offs, out):
+    nc = tc.nc
+    with (
+        tc.tile_pool(name="held", bufs=1) as held,
+        tc.psum_pool(name="psum", bufs=1) as psum,
+    ):
+        base_tile = held.tile([P, MB, S], BF16, name="base_tile")
+        offsets = held.tile([P, N // 16], U16, name="offsets")
+        w_tile = held.tile([P, KB, M], BF16, name="w_tile")
+        x_tile = held.tile([P, KB, N], BF16, name="x_tile")
+        out_tile = held.tile([P, MB, S], F32, name="out_tile")
+
+        nc.sync.dma_start(base_tile[:], base.rearrange("(b p) s -> p b s", p=P))
+        nc.sync.dma_start(offsets[:], offs)
+        nc.sync.dma_start(w_tile[:], w.rearrange("(p c) m -> p c m", c=KB))
+        nc.sync.dma_start(x_tile[:], x.rearrange("(p c) n -> p c n", c=KB))
+
+        identity = held.tile([P, P], BF16, name="identity")
+        make_identity(nc, identity[:])
+
+        windows = [psum.tile([P, S], F32, name=f"window{b}") for b in range(MB)]
+        for b in range(MB):
+            nc.tensor.matmul(windows[b][:], identity[:], base_tile[:, b, :], start=True, stop=False)
+
+        for b in range(MB):
+            for c in range(KB):
+                nc.tensor.matmul(
+                    windows[b][:].indirect(offsets[:]),
+                    w_tile[:, c, b * P : (b + 1) * P],
+                    x_tile[:, c, :],
+                    start=False,
+                    stop=c == KB - 1,
+                )
+
+        out_rows = out.rearrange("(b p) s -> p b s", p=P)
+        for b in range(MB):
+            nc.vector.tensor_copy(out_tile[:, b, :], windows[b][:])
+            nc.sync.dma_start(out_rows[:, b, :], out_tile[:, b, :])

@@ -8,6 +8,10 @@ K = 512
 M = 256
 KB = K // P
 MB = M // P
+HALVES = 2
+HB = KB // HALVES
+WARM = 512
+WARM_UPS = 4
 
 FLOPS = 2 * K * M * N
 
@@ -22,16 +26,24 @@ def tile_scatter_matmul_kernel(tc, base, x, w, offs, out):
         tc.tile_pool(name="held", bufs=1) as held,
         tc.psum_pool(name="psum", bufs=1) as psum,
     ):
+        zeros = held.tile([P, WARM], BF16, name="zeros")
+        nc.vector.memset(zeros[:], 0.0)
+        spare = psum.tile([P, WARM], F32, name="spare")
+        for warm_up in range(WARM_UPS):
+            nc.tensor.matmul(spare[:], zeros[:, :P], zeros[:], start=True, stop=True)
+
         base_tile = held.tile([P, MB, S], BF16, name="base_tile")
         offsets = held.tile([P, N // 16], U16, name="offsets")
-        w_tile = held.tile([P, KB, M], BF16, name="w_tile")
+        w_halves = [held.tile([P, HB, M], BF16, name=f"w_half{h}") for h in range(HALVES)]
         x_tile = held.tile([P, KB, N], BF16, name="x_tile")
         out_tile = held.tile([P, MB, S], F32, name="out_tile")
 
         nc.sync.dma_start(base_tile[:], base.rearrange("(b p) s -> p b s", p=P))
         nc.sync.dma_start(offsets[:], offs)
-        nc.sync.dma_start(w_tile[:], w.rearrange("(p c) m -> p c m", c=KB))
         nc.sync.dma_start(x_tile[:], x.rearrange("(p c) n -> p c n", c=KB))
+        w_rows = w.rearrange("(p c) m -> p c m", c=KB)
+        for h in range(HALVES):
+            nc.sync.dma_start(w_halves[h][:], w_rows[:, h * HB : (h + 1) * HB, :])
 
         identity = held.tile([P, P], BF16, name="identity")
         make_identity(nc, identity[:])
@@ -40,15 +52,17 @@ def tile_scatter_matmul_kernel(tc, base, x, w, offs, out):
         for b in range(MB):
             nc.tensor.matmul(windows[b][:], identity[:], base_tile[:, b, :], start=True, stop=False)
 
-        for b in range(MB):
-            for c in range(KB):
-                nc.tensor.matmul(
-                    windows[b][:].indirect(offsets[:]),
-                    w_tile[:, c, b * P : (b + 1) * P],
-                    x_tile[:, c, :],
-                    start=False,
-                    stop=c == KB - 1,
-                )
+        for h in range(HALVES):
+            for b in range(MB):
+                for i in range(HB):
+                    c = h * HB + i
+                    nc.tensor.matmul(
+                        windows[b][:].indirect(offsets[:]),
+                        w_halves[h][:, i, b * P : (b + 1) * P],
+                        x_tile[:, c, :],
+                        start=False,
+                        stop=c == KB - 1,
+                    )
 
         out_rows = out.rearrange("(b p) s -> p b s", p=P)
         for b in range(MB):

@@ -10,8 +10,8 @@ KB = K // P
 MB = M // P
 HALVES = 2
 HB = KB // HALVES
-WARM = 512
-WARM_UPS = 4
+WARM = 256
+WARM_UPS = 6
 
 FLOPS = 2 * K * M * N
 
@@ -27,7 +27,7 @@ def tile_scatter_matmul_kernel(tc, base, x, w, offs, out):
         tc.psum_pool(name="psum", bufs=1) as psum,
     ):
         zeros = held.tile([P, WARM], BF16, name="zeros")
-        nc.vector.memset(zeros[:], 0.0)
+        nc.gpsimd.memset(zeros[:], 0.0)
         spare = psum.tile([P, WARM], F32, name="spare")
         for warm_up in range(WARM_UPS):
             nc.tensor.matmul(spare[:], zeros[:, :P], zeros[:], start=True, stop=True)
@@ -40,10 +40,10 @@ def tile_scatter_matmul_kernel(tc, base, x, w, offs, out):
 
         nc.sync.dma_start(base_tile[:], base.rearrange("(b p) s -> p b s", p=P))
         nc.sync.dma_start(offsets[:], offs)
-        nc.sync.dma_start(x_tile[:], x.rearrange("(p c) n -> p c n", c=KB))
+        nc.scalar.dma_start(x_tile[:], x.rearrange("(p c) n -> p c n", c=KB))
         w_rows = w.rearrange("(p c) m -> p c m", c=KB)
         for h in range(HALVES):
-            nc.sync.dma_start(w_halves[h][:], w_rows[:, h * HB : (h + 1) * HB, :])
+            nc.scalar.dma_start(w_halves[h][:], w_rows[:, h * HB : (h + 1) * HB, :])
 
         identity = held.tile([P, P], BF16, name="identity")
         make_identity(nc, identity[:])

@@ -38,7 +38,7 @@ def tile_scatter_matmul_kernel(tc, base, x, w, offs, out):
         x_tile = held.tile([P, KB, N], BF16, name="x_tile")
         out_tile = held.tile([P, MB, S], F32, name="out_tile")
 
-        nc.sync.dma_start(base_tile[:], base.rearrange("(b p) s -> p b s", p=P))
+        nc.sync.dma_start(base_tile[:], base.rearrange("(p b) s -> p b s", p=P))
         nc.sync.dma_start(offsets[:], offs)
         nc.scalar.dma_start(x_tile[:], x.rearrange("(p c) n -> p c n", c=KB))
         w_rows = w.rearrange("(p c) m -> p c m", c=KB)
@@ -58,13 +58,13 @@ def tile_scatter_matmul_kernel(tc, base, x, w, offs, out):
                     c = h * HB + i
                     nc.tensor.matmul(
                         windows[b][:].indirect(offsets[:]),
-                        w_halves[h][:, i, b * P : (b + 1) * P],
+                        w_halves[h][:, i, b::MB],
                         x_tile[:, c, :],
                         start=False,
                         stop=c == KB - 1,
                     )
 
-        out_rows = out.rearrange("(b p) s -> p b s", p=P)
+        out_rows = out.rearrange("(p b) s -> p b s", p=P)
         for b in range(MB):
             nc.vector.tensor_copy(out_tile[:, b, :], windows[b][:])
             nc.sync.dma_start(out_rows[:, b, :], out_tile[:, b, :])

import concourse.mybir as mybir
from concourse.masks import make_identity

P = 128
S = 256
N = 192
K = 512
M = 256
KB = K // P
MB = M // P
HALVES = 2
HB = KB // HALVES
WARM = 256
WARM_UPS = 6

FLOPS = 2 * K * M * N

BF16 = mybir.dt.bfloat16
F32 = mybir.dt.float32
U16 = mybir.dt.uint16


def tile_scatter_matmul_kernel(tc, base, x, w, offs, out):
    nc = tc.nc
    with (
        tc.tile_pool(name="held", bufs=1) as held,
        tc.psum_pool(name="psum", bufs=1) as psum,
    ):
        zeros = held.tile([P, WARM], BF16, name="zeros")
        nc.gpsimd.memset(zeros[:], 0.0)
        spare = psum.tile([P, WARM], F32, name="spare")
        for warm_up in range(WARM_UPS):
            nc.tensor.matmul(spare[:], zeros[:, :P], zeros[:], start=True, stop=True)

        base_tile = held.tile([P, MB, S], BF16, name="base_tile")
        offsets = held.tile([P, N // 16], U16, name="offsets")
        w_halves = [held.tile([P, HB, M], BF16, name=f"w_half{h}") for h in range(HALVES)]
        x_tile = held.tile([P, KB, N], BF16, name="x_tile")
        out_tile = held.tile([P, MB, S], F32, name="out_tile")

        nc.sync.dma_start(base_tile[:], base.rearrange("(p b) s -> p b s", p=P))
        nc.sync.dma_start(offsets[:], offs)
        nc.scalar.dma_start(x_tile[:], x.rearrange("(p c) n -> p c n", c=KB))
        w_rows = w.rearrange("(p c) m -> p c m", c=KB)
        for h in range(HALVES):
            nc.scalar.dma_start(w_halves[h][:], w_rows[:, h * HB : (h + 1) * HB, :])

        identity = held.tile([P, P], BF16, name="identity")
        make_identity(nc, identity[:])

        windows = [psum.tile([P, S], F32, name=f"window{b}") for b in range(MB)]
        for b in range(MB):
            nc.tensor.matmul(windows[b][:], identity[:], base_tile[:, b, :], start=True, stop=False)

        for h in range(HALVES):
            for b in range(MB):
                for i in range(HB):
                    c = h * HB + i
                    nc.tensor.matmul(
                        windows[b][:].indirect(offsets[:]),
                        w_halves[h][:, i, b::MB],
                        x_tile[:, c, :],
                        start=False,
                        stop=c == KB - 1,
                    )

        out_rows = out.rearrange("(p b) s -> p b s", p=P)
        for b in range(MB):
            nc.vector.tensor_copy(out_tile[:, b, :], windows[b][:])
            nc.sync.dma_start(out_rows[:, b, :], out_tile[:, b, :])
